import numpy as np
import ml_dtypes


def mxq(x, axis, fmt="e4m3"):
    dtype, down = {"e4m3": (ml_dtypes.float8_e4m3fn, 7), "e5m2": (ml_dtypes.float8_e5m2, 14)}[fmt]
    v = np.moveaxis(np.asarray(x, np.float32).astype(ml_dtypes.bfloat16).astype(np.float64), axis, -1)
    blocks = v.reshape(v.shape[:-1] + (-1, 32))
    amax = np.abs(blocks).max(-1, keepdims=True)
    byte = np.maximum(np.where(amax > 0, np.frexp(amax)[1] - 1 + 127, 0) - down, 1)
    scale = np.exp2(byte - 127.0)
    codes = (blocks / scale).astype(np.float32).astype(dtype).astype(np.float64)
    return np.moveaxis((codes * scale).reshape(v.shape), -1, axis)


WIDE = False


def mx_kscale(k):
    if not WIDE:
        return np.ones(k)
    levels = np.array([30, -30])
    if k % 512:
        return np.exp2(np.random.permutation(np.resize(levels, k // 32))).repeat(32)
    a = np.empty((k // 512, 16))
    for p in range(k // 512):
        a[p, :8] = np.random.permutation(np.resize(levels, 8))
        for g in range(8):
            far = levels[np.abs(levels - a[p, g]) >= 10]
            a[p, g + 8] = far[np.random.randint(len(far))]
    return np.exp2(a.ravel()).repeat(32)


def f64(x):
    return np.asarray(x).astype(np.float64)


def striped(idx):
    return np.tile(np.asarray(idx).reshape(-1, 16).T, (8, 1)).astype(np.uint16)


def unstriped(offs):
    return offs[:16].T.reshape(-1).astype(np.int64)


E2M1 = np.array([0.0, 0.5, 1.0, 1.5, 2.0, 3.0, 4.0, 6.0, -0.0, -0.5, -1.0, -1.5, -2.0, -3.0, -4.0, -6.0])


def pack_weight(w, fmt):
    k, n = w.shape
    w = f64(np.asarray(w, np.float32).astype(ml_dtypes.bfloat16)).reshape(k // 32, 32, n)
    amax = np.abs(w).max(1)
    if fmt in ("e4m3", "e5m2"):
        byte = np.frexp(amax)[1] - 1 + 127 - (7 if fmt == "e4m3" else 14)
    else:
        mant, ex = np.frexp(amax / 6.0)
        byte = np.where(mant > 0.5, ex, ex - 1) + 127
    byte = np.clip(np.where(amax > 0, byte, 1), 1, 254)
    scaled = (w * np.exp2(127.0 - byte)[:, None, :]).reshape(k, n).astype(np.float32)
    by_word = np.ascontiguousarray(scaled.reshape(k // 512, 128, 4, n).transpose(0, 1, 3, 2))
    if fmt in ("e4m3", "e5m2"):
        words = by_word.astype(ml_dtypes.float8_e4m3fn if fmt == "e4m3" else ml_dtypes.float8_e5m2).view(np.uint8)
    else:
        c = by_word.astype(ml_dtypes.float4_e2m1fn).view(np.uint8) & 0xF
        words = (c[..., 0::2] | (c[..., 1::2] << 4)).reshape(k // 512, 128, 2 * n)
    return np.ascontiguousarray(words), np.ascontiguousarray(byte.astype(np.uint8).reshape(k // 512, 16, n))


def unpack_weight(words, scales, fmt):
    g, _, n = scales.shape
    words = np.ascontiguousarray(words).reshape(g, 128, n, -1)
    if fmt in ("e4m3", "e5m2"):
        vals = words.view(ml_dtypes.float8_e4m3fn if fmt == "e4m3" else ml_dtypes.float8_e5m2).astype(np.float64)
    else:
        nib = np.empty((g, 128, n, 4), np.uint8)
        nib[..., 0::2] = words & 0xF
        nib[..., 1::2] = words >> 4
        vals = E2M1[nib]
    vals = vals * np.repeat(np.exp2(scales.astype(np.float64) - 127.0), 8, axis=1)[..., None]
    return vals.transpose(0, 1, 3, 2).reshape(g * 512, n)


K, T, J, I, R, Q = 512, 512, 256, 256, 512, 512


def setup_inputs():
    n = np.random.standard_normal
    idx = np.random.permutation(T)[:J]
    idx2 = np.random.permutation(T)[:I]
    idx3 = np.random.permutation(Q)[:I]
    fk = mx_kscale(K)
    fr = mx_kscale(R)
    xtp = pack_weight(n((K, T)) / fk[:, None], "e4m3")
    wap = pack_weight(n((K, R)) * 0.5 / np.sqrt(K) * fk[:, None] * fr, "e2m1")
    wbp = pack_weight(n((K, R)) * 1 / np.sqrt(K) * fk[:, None] / fr, "e5m2")
    return {
        "xt_words": xtp[0],
        "xt_scales": xtp[1],
        "wa_words": wap[0],
        "wa_scales": wap[1],
        "wb_words": wbp[0],
        "wb_scales": wbp[1],
        "ob": (n((R, I)) * 0.5 / fr[:, None]).astype(np.float32),
        "tv": (1.0 * n((J, Q))).astype(np.float32),
        "offs": striped(idx),
        "offs2": striped(idx2),
        "offs3": striped(idx3),
    }


def reference(xt_words, xt_scales, wa_words, wa_scales, wb_words, wb_scales, ob, tv, offs, offs2, offs3):
    idx = unstriped(offs)
    idx2 = unstriped(offs2)
    idx3 = unstriped(offs3)
    xtu = unpack_weight(xt_words, xt_scales, "e4m3")
    wau = unpack_weight(wa_words, wa_scales, "e2m1")
    wbu = unpack_weight(wb_words, wb_scales, "e5m2")
    xtidxg = xtu[:, idx]
    za = wau.T @ xtidxg
    ka1 = np.max(za, axis=1, keepdims=True)
    ha = np.maximum(za - 0.4 * ka1, 0.0)
    xtidx2g = xtu[:, idx2]
    zb = wbu.T @ xtidx2g
    hb = np.maximum(zb, f64(ob))
    haq = mxq(ha, 0, "e4m3")
    hbq = mxq(hb, 0, "e5m2")
    a0 = haq.T @ hbq
    y = np.tanh(0.04 * a0) * f64(tv)[:, idx3]
    return y

@@ -1,0 +1,176 @@
+from contextlib import ExitStack
+
+import concourse.mybir as mybir
+
+K, T, J, I, R, Q = 512, 512, 256, 256, 512, 512
+FLOPS = 2 * K * R * J + 2 * K * R * I + 2 * R * J * I
+
+F32 = mybir.dt.float32
+BF16 = mybir.dt.bfloat16
+I32 = mybir.dt.int32
+U32 = mybir.dt.uint32
+U16 = mybir.dt.uint16
+U8 = mybir.dt.uint8
+E4M3 = mybir.dt.float8_e4m3fn_x4
+E5M2 = mybir.dt.float8_e5m2_x4
+E2M1 = mybir.dt.float4_e2m1fn_x4
+ACT = mybir.ActivationFunctionType
+ALU = mybir.AluOpType
+
+P = 128
+PACK = 4
+RUN = 4
+HALF = 128
+
+
+def load_scale_rows(queue, plane_words, scales):
+    rows = scales[0].bitcast(I32)
+    for quad in range(4):
+        queue.dma_start(out=plane_words[32 * quad : 32 * quad + 4, :], in_=rows[4 * quad : 4 * quad + 4, :])
+
+
+def deal_columns(nc, dealt, raw, words_per_run):
+    nc.vector.tensor_copy(
+        out=dealt.rearrange("p (t g w) -> p g t w", t=PACK, w=words_per_run),
+        in_=raw.rearrange("p (g t w) -> p g t w", t=PACK, w=words_per_run),
+    )
+
+
+def tile_list_meet_peakgated_added_tabled_kernel(
+    tc, xt_words, xt_scales, wa_words, wa_scales, wb_words, wb_scales, ob, tv, offs, offs2, offs3, out
+):
+    nc = tc.nc
+    with ExitStack() as ctx:
+        sb = ctx.enter_context(tc.tile_pool(name="sb", bufs=1))
+        ps = ctx.enter_context(tc.psum_pool(name="ps", bufs=1))
+
+        rows_list = sb.tile([P, J // 16], U16, name="rows_list")
+        cols_list = sb.tile([P, I // 16], U16, name="cols_list")
+        tv_list = sb.tile([P, I // 16], U16, name="tv_list")
+        xt_w = sb.tile([P, T], I32, name="xt_w", align_bytes=64)
+        xt_s = sb.tile([P, T // 4], I32, name="xt_s", align_bytes=64)
+        wa_w_raw = sb.tile([P, R // 2], I32, name="wa_w_raw", align_bytes=64)
+        wb_w_raw = sb.tile([P, R], I32, name="wb_w_raw", align_bytes=64)
+        wa_s_raw = sb.tile([P, R // 4], I32, name="wa_s_raw", align_bytes=64)
+        wb_s_raw = sb.tile([P, R // 4], I32, name="wb_s_raw", align_bytes=64)
+        ob_sb = sb.tile([P, PACK, I], F32, name="ob_sb", align_bytes=64)
+        tv_sb = [sb.tile([P, Q], F32, name="tv_sb%d" % h, align_bytes=64) for h in range(2)]
+
+        nc.vector.memset(xt_s[:], 0)
+        nc.vector.memset(wa_s_raw[:], 0)
+        nc.vector.memset(wb_s_raw[:], 0)
+
+        nc.sync.dma_start(rows_list[:], offs)
+        nc.sync.dma_start(out=xt_w[:], in_=xt_words[0].rearrange("p n t -> p (n t)").bitcast(I32))
+        nc.sync.dma_start(cols_list[:], offs2)
+        load_scale_rows(nc.scalar, xt_s, xt_scales)
+        nc.sync.dma_start(out=wa_w_raw[:], in_=wa_words[0].bitcast(I32))
+        load_scale_rows(nc.sync, wa_s_raw, wa_scales)
+        nc.sync.dma_start(out=wb_w_raw[:], in_=wb_words[0].rearrange("p n t -> p (n t)").bitcast(I32))
+        load_scale_rows(nc.sync, wb_s_raw, wb_scales)
+        ob_runs = ob.rearrange("(g t e) i -> e g t i", t=PACK, e=RUN)
+        for e in range(RUN):
+            nc.sync.dma_start(out=ob_sb[e:P:RUN, :, :], in_=ob_runs[e])
+        nc.sync.dma_start(tv_list[:], offs3)
+        for h in range(2):
+            nc.sync.dma_start(out=tv_sb[h][:], in_=tv[h * HALF : (h + 1) * HALF, :])
+
+        xa_w = sb.tile([P, J], U32, name="xa_w", align_bytes=64)
+        xa_s = sb.tile([P, J], U8, name="xa_s", align_bytes=64)
+        xb_w = sb.tile([P, I], U32, name="xb_w", align_bytes=64)
+        xb_s = sb.tile([P, I], U8, name="xb_s", align_bytes=64)
+        wa_w = sb.tile([P, R // 2], I32, name="wa_w", align_bytes=64)
+        wb_w = sb.tile([P, R], I32, name="wb_w", align_bytes=64)
+        wa_s = sb.tile([P, R // 4], I32, name="wa_s", align_bytes=64)
+        wb_s = sb.tile([P, R // 4], I32, name="wb_s", align_bytes=64)
+
+        nc.vector.tensor_copy(xa_w[:], xt_w[:].bitcast(U32).indirect(rows_list[:]))
+        nc.vector.tensor_copy(xa_s[:], xt_s[:].bitcast(U8).indirect(rows_list[:]))
+        deal_columns(nc, wa_w[:], wa_w_raw[:], 2)
+        deal_columns(nc, wa_s[:], wa_s_raw[:], 1)
+        nc.vector.tensor_copy(xb_w[:], xt_w[:].bitcast(U32).indirect(cols_list[:]))
+        nc.vector.tensor_copy(xb_s[:], xt_s[:].bitcast(U8).indirect(cols_list[:]))
+        deal_columns(nc, wb_w[:], wb_w_raw[:], 4)
+        deal_columns(nc, wb_s[:], wb_s_raw[:], 1)
+
+        za = [ps.tile([P, 2, J], F32, name="za%d" % b) for b in range(2)]
+        for t in range(PACK):
+            nc.tensor.matmul_mx(
+                out=za[t // 2][:, t % 2, :],
+                lhsT=wa_w[:].bitcast(U8)[:, 2 * P * t : 2 * P * (t + 1)].bitcast(E2M1),
+                lhsT_scale=wa_s[:].bitcast(U8)[:, P * t : P * (t + 1)],
+                rhs=xa_w[:].bitcast(E4M3),
+                rhs_scale=xa_s[:],
+                start=True,
+                stop=True,
+            )
+        zb = [ps.tile([P, PACK, HALF], F32, name="zb%d" % h) for h in range(2)]
+        for h in range(2):
+            cols = slice(h * HALF, (h + 1) * HALF)
+            for t in range(PACK):
+                nc.tensor.matmul_mx(
+                    out=zb[h][:, t, :],
+                    lhsT=wb_w[:, P * t : P * (t + 1)].bitcast(E5M2),
+                    lhsT_scale=wb_s[:].bitcast(U8)[:, P * t : P * (t + 1)],
+                    rhs=xb_w[:, cols].bitcast(E4M3),
+                    rhs_scale=xb_s[:, cols],
+                    start=True,
+                    stop=True,
+                )
+
+        ha_flat = sb.tile([P, PACK, J], BF16, name="ha_flat", align_bytes=64)
+        for b in range(2):
+            peak = sb.tile([P, 2], F32, name="peak%d" % b)
+            gate = sb.tile([P, 2], F32, name="gate%d" % b)
+            nc.vector.tensor_reduce(out=peak[:], in_=za[b][:], axis=mybir.AxisListType.X, op=ALU.max)
+            nc.scalar.mul(gate[:], peak[:], -0.4)
+            for u in range(2):
+                nc.scalar.activation(ha_flat[:, 2 * b + u, :], za[b][:, u, :], ACT.Relu, bias=gate[:, u : u + 1])
+
+        hb = sb.tile([P, I, PACK], BF16, name="hb", align_bytes=64)
+        for h in range(2):
+            cols = slice(h * HALF, (h + 1) * HALF)
+            nc.vector.tensor_tensor(
+                out=hb[:, cols, :].rearrange("p (c e) t -> p c t e", e=4),
+                in0=zb[h][:].rearrange("p t (c e) -> p c t e", e=4),
+                in1=ob_sb[:, :, cols].rearrange("p t (c e) -> p c t e", e=4),
+                op=ALU.max,
+            )
+        hb_w = sb.tile([P, I], U32, name="hb_w", align_bytes=64)
+        hb_s = sb.tile([P, I], U8, name="hb_s", align_bytes=64)
+        nc.vector.quantize_mx(out=hb_w[:].bitcast(E5M2), scales=hb_s[:], in_=hb[:].rearrange("p i t -> p (i t)"))
+
+        tv_g = []
+        for h in range(2):
+            picked = sb.tile([P, I], F32, name="tv_g%d" % h, align_bytes=64)
+            nc.scalar.activation(picked[:], tv_sb[h][:].indirect(tv_list[:]), ACT.Copy)
+            tv_g.append(picked)
+
+        ha = []
+        for h in range(2):
+            rows = slice(h * HALF, (h + 1) * HALF)
+            woven = sb.tile([P, HALF, PACK], BF16, name="ha%d" % h, align_bytes=64)
+            nc.vector.tensor_copy(
+                out=woven[:].rearrange("p (c e) t -> p c t e", e=4),
+                in_=ha_flat[:, :, rows].rearrange("p t (c e) -> p c t e", e=4),
+            )
+            ha.append(woven)
+        for h in range(2):
+            ha_w = sb.tile([P, HALF], U32, name="ha_w%d" % h, align_bytes=64)
+            ha_s = sb.tile([P, HALF], U8, name="ha_s%d" % h, align_bytes=64)
+            nc.vector.quantize_mx(out=ha_w[:].bitcast(E4M3), scales=ha_s[:], in_=ha[h][:].rearrange("p j t -> p (j t)"))
+            score = ps.tile([P, I], F32, name="score%d" % h)
+            nc.tensor.matmul_mx(
+                out=score[:],
+                lhsT=ha_w[:].bitcast(E4M3),
+                lhsT_scale=ha_s[:],
+                rhs=hb_w[:].bitcast(E5M2),
+                rhs_scale=hb_s[:],
+                start=True,
+                stop=True,
+            )
+            bent = sb.tile([P, I], F32, name="bent%d" % h, align_bytes=64)
+            nc.scalar.activation(bent[:], score[:], ACT.Tanh, scale=0.04)
+            y = sb.tile([P, I], F32, name="y%d" % h, align_bytes=64)
+            nc.vector.tensor_tensor(out=y[:], in0=bent[:], in1=tv_g[h][:], op=ALU.mult)
+            nc.sync.dma_start(out=out[h * HALF : (h + 1) * HALF, :], in_=y[:])

@@ -23,10 +23,10 @@ RUN = 4
 HALF = 128
 
 
-def load_scale_rows(queue, plane_words, scales):
+def load_scale_rows(queues, plane_words, scales):
     rows = scales[0].bitcast(I32)
     for quad in range(4):
-        queue.dma_start(out=plane_words[32 * quad : 32 * quad + 4, :], in_=rows[4 * quad : 4 * quad + 4, :])
+        queues[quad % len(queues)].dma_start(out=plane_words[32 * quad : 32 * quad + 4, :], in_=rows[4 * quad : 4 * quad + 4, :])
 
 
 def deal_columns(nc, dealt, raw, words_per_run):
@@ -51,47 +51,47 @@ def tile_list_meet_peakgated_added_tabled_kernel(
         xt_s = sb.tile([P, T // 4], I32, name="xt_s", align_bytes=64)
         wa_w_raw = sb.tile([P, R // 2], I32, name="wa_w_raw", align_bytes=64)
         wb_w_raw = sb.tile([P, R], I32, name="wb_w_raw", align_bytes=64)
-        wa_s_raw = sb.tile([P, R // 4], I32, name="wa_s_raw", align_bytes=64)
-        wb_s_raw = sb.tile([P, R // 4], I32, name="wb_s_raw", align_bytes=64)
-        ob_sb = sb.tile([P, PACK, I], F32, name="ob_sb", align_bytes=64)
-        tv_sb = [sb.tile([P, Q], F32, name="tv_sb%d" % h, align_bytes=64) for h in range(2)]
+        wa_s_raw = sb.tile([P, R // 4], I32, name="wa_s_raw", tag="wa_s_raw_then_xb_s", align_bytes=64)
+        wb_s_raw = sb.tile([P, R // 4], I32, name="wb_s_raw", tag="wb_s_raw_then_peak", align_bytes=64)
+        ob_sb = sb.tile([P, PACK, I], F32, name="ob_sb", tag="ob_then_ha", align_bytes=64)
+        tv_sb = sb.tile([P, 2, Q], F32, name="tv_sb", align_bytes=64)
 
         nc.vector.memset(xt_s[:], 0)
-        nc.vector.memset(wa_s_raw[:], 0)
-        nc.vector.memset(wb_s_raw[:], 0)
+        nc.gpsimd.memset(wa_s_raw[:], 0)
+        nc.gpsimd.memset(wb_s_raw[:], 0)
 
         nc.sync.dma_start(rows_list[:], offs)
-        nc.sync.dma_start(out=xt_w[:], in_=xt_words[0].rearrange("p n t -> p (n t)").bitcast(I32))
+        nc.scalar.dma_start(out=xt_w[:], in_=xt_words[0].rearrange("p n t -> p (n t)").bitcast(I32))
         nc.sync.dma_start(cols_list[:], offs2)
-        load_scale_rows(nc.scalar, xt_s, xt_scales)
-        nc.sync.dma_start(out=wa_w_raw[:], in_=wa_words[0].bitcast(I32))
-        load_scale_rows(nc.sync, wa_s_raw, wa_scales)
-        nc.sync.dma_start(out=wb_w_raw[:], in_=wb_words[0].rearrange("p n t -> p (n t)").bitcast(I32))
-        load_scale_rows(nc.sync, wb_s_raw, wb_scales)
+        nc.scalar.dma_start(out=wa_w_raw[:], in_=wa_words[0].bitcast(I32))
+        load_scale_rows([nc.sync, nc.scalar], xt_s, xt_scales)
+        load_scale_rows([nc.sync, nc.scalar, nc.sync, nc.gpsimd], wa_s_raw, wa_scales)
+        load_scale_rows([nc.scalar, nc.sync], wb_s_raw, wb_scales)
+        nc.scalar.dma_start(out=wb_w_raw[:], in_=wb_words[0].rearrange("p n t -> p (n t)").bitcast(I32))
         ob_runs = ob.rearrange("(g t e) i -> e g t i", t=PACK, e=RUN)
         for e in range(RUN):
-            nc.sync.dma_start(out=ob_sb[e:P:RUN, :, :], in_=ob_runs[e])
+            queue = nc.gpsimd if e == RUN - 1 else nc.sync
+            queue.dma_start(out=ob_sb[e:P:RUN, :, :], in_=ob_runs[e])
         nc.sync.dma_start(tv_list[:], offs3)
-        for h in range(2):
-            nc.sync.dma_start(out=tv_sb[h][:], in_=tv[h * HALF : (h + 1) * HALF, :])
+        nc.sync.dma_start(out=tv_sb[:], in_=tv.rearrange("(h p) q -> p h q", p=P))
 
         xa_w = sb.tile([P, J], U32, name="xa_w", align_bytes=64)
         xa_s = sb.tile([P, J], U8, name="xa_s", align_bytes=64)
         xb_w = sb.tile([P, I], U32, name="xb_w", align_bytes=64)
-        xb_s = sb.tile([P, I], U8, name="xb_s", align_bytes=64)
         wa_w = sb.tile([P, R // 2], I32, name="wa_w", align_bytes=64)
         wb_w = sb.tile([P, R], I32, name="wb_w", align_bytes=64)
         wa_s = sb.tile([P, R // 4], I32, name="wa_s", align_bytes=64)
         wb_s = sb.tile([P, R // 4], I32, name="wb_s", align_bytes=64)
 
         nc.vector.tensor_copy(xa_w[:], xt_w[:].bitcast(U32).indirect(rows_list[:]))
+        nc.vector.tensor_copy(xb_w[:], xt_w[:].bitcast(U32).indirect(cols_list[:]))
         nc.vector.tensor_copy(xa_s[:], xt_s[:].bitcast(U8).indirect(rows_list[:]))
         deal_columns(nc, wa_w[:], wa_w_raw[:], 2)
         deal_columns(nc, wa_s[:], wa_s_raw[:], 1)
-        nc.vector.tensor_copy(xb_w[:], xt_w[:].bitcast(U32).indirect(cols_list[:]))
+        xb_s = sb.tile([P, I], U8, name="xb_s", tag="wa_s_raw_then_xb_s", align_bytes=64)
         nc.vector.tensor_copy(xb_s[:], xt_s[:].bitcast(U8).indirect(cols_list[:]))
-        deal_columns(nc, wb_w[:], wb_w_raw[:], 4)
         deal_columns(nc, wb_s[:], wb_s_raw[:], 1)
+        deal_columns(nc, wb_w[:], wb_w_raw[:], 4)
 
         za = [ps.tile([P, 2, J], F32, name="za%d" % b) for b in range(2)]
         for t in range(PACK):
@@ -119,13 +119,16 @@ def tile_list_meet_peakgated_added_tabled_kernel(
                 )
 
         ha_flat = sb.tile([P, PACK, J], BF16, name="ha_flat", align_bytes=64)
+        peak = sb.tile([P, PACK], F32, name="peak", tag="wb_s_raw_then_peak", align_bytes=64)
+        gates = []
         for b in range(2):
-            peak = sb.tile([P, 2], F32, name="peak%d" % b)
-            gate = sb.tile([P, 2], F32, name="gate%d" % b)
-            nc.vector.tensor_reduce(out=peak[:], in_=za[b][:], axis=mybir.AxisListType.X, op=ALU.max)
-            nc.scalar.mul(gate[:], peak[:], -0.4)
-            for u in range(2):
-                nc.scalar.activation(ha_flat[:, 2 * b + u, :], za[b][:, u, :], ACT.Relu, bias=gate[:, u : u + 1])
+            gate = sb.tile([P, 2], F32, name="gate%d" % b, tag="gate_then_tv%d" % b, align_bytes=64)
+            nc.vector.tensor_reduce(out=peak[:, 2 * b : 2 * b + 2], in_=za[b][:], axis=mybir.AxisListType.X, op=ALU.max)
+            nc.scalar.mul(gate[:], peak[:, 2 * b : 2 * b + 2], -0.4)
+            gates.append(gate)
+        for t in range(PACK):
+            b, u = divmod(t, 2)
+            nc.scalar.activation(ha_flat[:, t, :], za[b][:, u, :], ACT.Relu, bias=gates[b][:, u : u + 1])
 
         hb = sb.tile([P, I, PACK], BF16, name="hb", align_bytes=64)
         for h in range(2):
@@ -138,27 +141,27 @@ def tile_list_meet_peakgated_added_tabled_kernel(
             )
         hb_w = sb.tile([P, I], U32, name="hb_w", align_bytes=64)
         hb_s = sb.tile([P, I], U8, name="hb_s", align_bytes=64)
-        nc.vector.quantize_mx(out=hb_w[:].bitcast(E5M2), scales=hb_s[:], in_=hb[:].rearrange("p i t -> p (i t)"))
 
         tv_g = []
         for h in range(2):
-            picked = sb.tile([P, I], F32, name="tv_g%d" % h, align_bytes=64)
-            nc.scalar.activation(picked[:], tv_sb[h][:].indirect(tv_list[:]), ACT.Copy)
+            picked = sb.tile([P, I], F32, name="tv_g%d" % h, tag="gate_then_tv%d" % h, align_bytes=64)
+            nc.scalar.activation(picked[:], tv_sb[:, h, :].indirect(tv_list[:]), ACT.Copy)
             tv_g.append(picked)
 
-        ha = []
+        ha = sb.tile([P, J, PACK], BF16, name="ha", tag="ob_then_ha", align_bytes=64)
         for h in range(2):
             rows = slice(h * HALF, (h + 1) * HALF)
-            woven = sb.tile([P, HALF, PACK], BF16, name="ha%d" % h, align_bytes=64)
+            nc.vector.quantize_mx(
+                out=hb_w[:, rows].bitcast(E5M2), scales=hb_s[:, rows], in_=hb[:, rows, :].rearrange("p i t -> p (i t)")
+            )
             nc.vector.tensor_copy(
-                out=woven[:].rearrange("p (c e) t -> p c t e", e=4),
+                out=ha[:, rows, :].rearrange("p (c e) t -> p c t e", e=4),
                 in_=ha_flat[:, :, rows].rearrange("p t (c e) -> p c t e", e=4),
             )
-            ha.append(woven)
         for h in range(2):
             ha_w = sb.tile([P, HALF], U32, name="ha_w%d" % h, align_bytes=64)
             ha_s = sb.tile([P, HALF], U8, name="ha_s%d" % h, align_bytes=64)
-            nc.vector.quantize_mx(out=ha_w[:].bitcast(E4M3), scales=ha_s[:], in_=ha[h][:].rearrange("p j t -> p (j t)"))
+            nc.vector.quantize_mx(out=ha_w[:].bitcast(E4M3), scales=ha_s[:], in_=ha[:, h * HALF : (h + 1) * HALF, :].rearrange("p j t -> p (j t)"))
             score = ps.tile([P, I], F32, name="score%d" % h)
             nc.tensor.matmul_mx(
                 out=score[:],

@@ -21,12 +21,19 @@ P = 128
 PACK = 4
 RUN = 4
 HALF = 128
+LIST_ROWS = 16
+ALIGN = 64
+STRIDE_READ = 4
 
 
-def load_scale_rows(queues, plane_words, scales):
+def halves():
+    return [(h, slice(h * HALF, (h + 1) * HALF)) for h in range(2)]
+
+
+def load_scale_rows(queues, plane, scales):
     rows = scales[0].bitcast(I32)
-    for quad in range(4):
-        queues[quad % len(queues)].dma_start(out=plane_words[32 * quad : 32 * quad + 4, :], in_=rows[4 * quad : 4 * quad + 4, :])
+    for n in range(4):
+        queues[n % len(queues)].dma_start(out=plane[32 * n : 32 * n + 4, :], in_=rows[4 * n : 4 * n + 4, :])
 
 
 def deal_columns(nc, dealt, raw, words_per_run):
@@ -44,17 +51,17 @@ def tile_list_meet_peakgated_added_tabled_kernel(
         sb = ctx.enter_context(tc.tile_pool(name="sb", bufs=1))
         ps = ctx.enter_context(tc.psum_pool(name="ps", bufs=1))
 
-        rows_list = sb.tile([P, J // 16], U16, name="rows_list")
-        cols_list = sb.tile([P, I // 16], U16, name="cols_list")
-        tv_list = sb.tile([P, I // 16], U16, name="tv_list")
-        xt_w = sb.tile([P, T], I32, name="xt_w", align_bytes=64)
-        xt_s = sb.tile([P, T // 4], I32, name="xt_s", align_bytes=64)
-        wa_w_raw = sb.tile([P, R // 2], I32, name="wa_w_raw", align_bytes=64)
-        wb_w_raw = sb.tile([P, R], I32, name="wb_w_raw", align_bytes=64)
-        wa_s_raw = sb.tile([P, R // 4], I32, name="wa_s_raw", tag="wa_s_raw_then_xb_s", align_bytes=64)
-        wb_s_raw = sb.tile([P, R // 4], I32, name="wb_s_raw", tag="wb_s_raw_then_peak", align_bytes=64)
-        ob_sb = sb.tile([P, PACK, I], F32, name="ob_sb", tag="ob_then_ha", align_bytes=64)
-        tv_sb = sb.tile([P, 2, Q], F32, name="tv_sb", align_bytes=64)
+        rows_list = sb.tile([P, J // LIST_ROWS], U16, name="rows_list")
+        cols_list = sb.tile([P, I // LIST_ROWS], U16, name="cols_list")
+        tv_list = sb.tile([P, I // LIST_ROWS], U16, name="tv_list")
+        xt_w = sb.tile([P, T], I32, name="xt_w", align_bytes=ALIGN)
+        xt_s = sb.tile([P, T // 4], I32, name="xt_s", align_bytes=ALIGN)
+        wa_w_raw = sb.tile([P, R // 2], I32, name="wa_w_raw", align_bytes=ALIGN)
+        wb_w_raw = sb.tile([P, R], I32, name="wb_w_raw", align_bytes=ALIGN)
+        wa_s_raw = sb.tile([P, R // 4], I32, name="wa_s_raw", tag="wa_s_raw_then_xb_s", align_bytes=ALIGN)
+        wb_s_raw = sb.tile([P, R // 4], I32, name="wb_s_raw", tag="wb_s_raw_then_peak", align_bytes=ALIGN)
+        ob_sb = sb.tile([P, PACK, I], F32, name="ob_sb", tag="ob_then_ha", align_bytes=ALIGN)
+        tv_sb = sb.tile([P, 2, Q], F32, name="tv_sb", align_bytes=ALIGN)
 
         nc.vector.memset(xt_s[:], 0)
         nc.gpsimd.memset(wa_s_raw[:], 0)
@@ -69,29 +76,28 @@ def tile_list_meet_peakgated_added_tabled_kernel(
         load_scale_rows([nc.scalar, nc.sync], wb_s_raw, wb_scales)
         nc.scalar.dma_start(out=wb_w_raw[:], in_=wb_words[0].rearrange("p n t -> p (n t)").bitcast(I32))
         ob_runs = ob.rearrange("(g t e) i -> e g t i", t=PACK, e=RUN)
-        for e in range(RUN):
-            queue = nc.gpsimd if e == RUN - 1 else nc.sync
+        for e, queue in enumerate([nc.sync, nc.sync, nc.sync, nc.gpsimd]):
             queue.dma_start(out=ob_sb[e:P:RUN, :, :], in_=ob_runs[e])
         nc.sync.dma_start(tv_list[:], offs3)
         nc.sync.dma_start(out=tv_sb[:], in_=tv.rearrange("(h p) q -> p h q", p=P))
 
-        xa_w = sb.tile([P, J], U32, name="xa_w", align_bytes=64)
-        xa_s = sb.tile([P, J], U8, name="xa_s", align_bytes=64)
-        xb_w = sb.tile([P, I], U32, name="xb_w", align_bytes=64)
-        wa_w = sb.tile([P, R // 2], I32, name="wa_w", align_bytes=64)
-        wb_w = sb.tile([P, R], I32, name="wb_w", align_bytes=64)
-        wa_s = sb.tile([P, R // 4], I32, name="wa_s", align_bytes=64)
-        wb_s = sb.tile([P, R // 4], I32, name="wb_s", align_bytes=64)
+        xa_w = sb.tile([P, J], U32, name="xa_w", align_bytes=ALIGN)
+        xa_s = sb.tile([P, J], U8, name="xa_s", align_bytes=ALIGN)
+        xb_w = sb.tile([P, I], U32, name="xb_w", align_bytes=ALIGN)
+        wa_w = sb.tile([P, R // 2], I32, name="wa_w", align_bytes=ALIGN)
+        wb_w = sb.tile([P, R], I32, name="wb_w", align_bytes=ALIGN)
+        wa_s = sb.tile([P, R // 4], I32, name="wa_s", align_bytes=ALIGN)
+        wb_s = sb.tile([P, R // 4], I32, name="wb_s", align_bytes=ALIGN)
 
         nc.vector.tensor_copy(xa_w[:], xt_w[:].bitcast(U32).indirect(rows_list[:]))
         nc.vector.tensor_copy(xb_w[:], xt_w[:].bitcast(U32).indirect(cols_list[:]))
         nc.vector.tensor_copy(xa_s[:], xt_s[:].bitcast(U8).indirect(rows_list[:]))
-        deal_columns(nc, wa_w[:], wa_w_raw[:], 2)
-        deal_columns(nc, wa_s[:], wa_s_raw[:], 1)
-        xb_s = sb.tile([P, I], U8, name="xb_s", tag="wa_s_raw_then_xb_s", align_bytes=64)
+        deal_columns(nc, wa_w[:], wa_w_raw[:], RUN // 2)
+        deal_columns(nc, wa_s[:], wa_s_raw[:], RUN // 4)
+        xb_s = sb.tile([P, I], U8, name="xb_s", tag="wa_s_raw_then_xb_s", align_bytes=ALIGN)
         nc.vector.tensor_copy(xb_s[:], xt_s[:].bitcast(U8).indirect(cols_list[:]))
-        deal_columns(nc, wb_s[:], wb_s_raw[:], 1)
-        deal_columns(nc, wb_w[:], wb_w_raw[:], 4)
+        deal_columns(nc, wb_s[:], wb_s_raw[:], RUN // 4)
+        deal_columns(nc, wb_w[:], wb_w_raw[:], RUN)
 
         za = [ps.tile([P, 2, J], F32, name="za%d" % b) for b in range(2)]
         for t in range(PACK):
@@ -104,12 +110,11 @@ def tile_list_meet_peakgated_added_tabled_kernel(
                 start=True,
                 stop=True,
             )
-        zb = [ps.tile([P, PACK, HALF], F32, name="zb%d" % h) for h in range(2)]
-        for h in range(2):
-            cols = slice(h * HALF, (h + 1) * HALF)
+        zb = [ps.tile([P, PACK, HALF], F32, name="zb%d" % c) for c in range(2)]
+        for c, cols in halves():
             for t in range(PACK):
                 nc.tensor.matmul_mx(
-                    out=zb[h][:, t, :],
+                    out=zb[c][:, t, :],
                     lhsT=wb_w[:, P * t : P * (t + 1)].bitcast(E5M2),
                     lhsT_scale=wb_s[:].bitcast(U8)[:, P * t : P * (t + 1)],
                     rhs=xb_w[:, cols].bitcast(E4M3),
@@ -118,11 +123,11 @@ def tile_list_meet_peakgated_added_tabled_kernel(
                     stop=True,
                 )
 
-        ha_flat = sb.tile([P, PACK, J], BF16, name="ha_flat", align_bytes=64)
-        peak = sb.tile([P, PACK], F32, name="peak", tag="wb_s_raw_then_peak", align_bytes=64)
+        ha_flat = sb.tile([P, PACK, J], BF16, name="ha_flat", align_bytes=ALIGN)
+        peak = sb.tile([P, PACK], F32, name="peak", tag="wb_s_raw_then_peak", align_bytes=ALIGN)
         gates = []
         for b in range(2):
-            gate = sb.tile([P, 2], F32, name="gate%d" % b, tag="gate_then_tv%d" % b, align_bytes=64)
+            gate = sb.tile([P, 2], F32, name="gate%d" % b, tag="gate_then_tv%d" % b, align_bytes=ALIGN)
             nc.vector.tensor_reduce(out=peak[:, 2 * b : 2 * b + 2], in_=za[b][:], axis=mybir.AxisListType.X, op=ALU.max)
             nc.scalar.mul(gate[:], peak[:, 2 * b : 2 * b + 2], -0.4)
             gates.append(gate)
@@ -130,50 +135,59 @@ def tile_list_meet_peakgated_added_tabled_kernel(
             b, u = divmod(t, 2)
             nc.scalar.activation(ha_flat[:, t, :], za[b][:, u, :], ACT.Relu, bias=gates[b][:, u : u + 1])
 
-        hb = sb.tile([P, I, PACK], BF16, name="hb", align_bytes=64)
-        for h in range(2):
-            cols = slice(h * HALF, (h + 1) * HALF)
+        hb = sb.tile([P, I, PACK], BF16, name="hb", align_bytes=ALIGN)
+        for c, cols in halves():
             nc.vector.tensor_tensor(
-                out=hb[:, cols, :].rearrange("p (c e) t -> p c t e", e=4),
-                in0=zb[h][:].rearrange("p t (c e) -> p c t e", e=4),
-                in1=ob_sb[:, :, cols].rearrange("p t (c e) -> p c t e", e=4),
+                out=hb[:, cols, :].rearrange("p (m n) t -> p m t n", n=STRIDE_READ),
+                in0=zb[c][:].rearrange("p t (m n) -> p m t n", n=STRIDE_READ),
+                in1=ob_sb[:, :, cols].rearrange("p t (m n) -> p m t n", n=STRIDE_READ),
                 op=ALU.max,
             )
-        hb_w = sb.tile([P, I], U32, name="hb_w", align_bytes=64)
-        hb_s = sb.tile([P, I], U8, name="hb_s", align_bytes=64)
+        hb_w = sb.tile([P, I], U32, name="hb_w", align_bytes=ALIGN)
+        hb_s = sb.tile([P, I], U8, name="hb_s", align_bytes=ALIGN)
 
-        tv_g = []
-        for h in range(2):
-            picked = sb.tile([P, I], F32, name="tv_g%d" % h, tag="gate_then_tv%d" % h, align_bytes=64)
-            nc.scalar.activation(picked[:], tv_sb[:, h, :].indirect(tv_list[:]), ACT.Copy)
-            tv_g.append(picked)
-
-        ha = sb.tile([P, J, PACK], BF16, name="ha", tag="ob_then_ha", align_bytes=64)
-        for h in range(2):
-            rows = slice(h * HALF, (h + 1) * HALF)
+        def quantize_hb(cols):
             nc.vector.quantize_mx(
-                out=hb_w[:, rows].bitcast(E5M2), scales=hb_s[:, rows], in_=hb[:, rows, :].rearrange("p i t -> p (i t)")
+                out=hb_w[:, cols].bitcast(E5M2), scales=hb_s[:, cols], in_=hb[:, cols, :].rearrange("p i t -> p (i t)")
             )
-            nc.vector.tensor_copy(
-                out=ha[:, rows, :].rearrange("p (c e) t -> p c t e", e=4),
-                in_=ha_flat[:, :, rows].rearrange("p t (c e) -> p c t e", e=4),
-            )
+
+        first_cols, second_cols = [cols for c, cols in halves()]
+        quantize_hb(first_cols)
+
+        tv_picked = []
         for h in range(2):
-            ha_w = sb.tile([P, HALF], U32, name="ha_w%d" % h, align_bytes=64)
-            ha_s = sb.tile([P, HALF], U8, name="ha_s%d" % h, align_bytes=64)
-            nc.vector.quantize_mx(out=ha_w[:].bitcast(E4M3), scales=ha_s[:], in_=ha[:, h * HALF : (h + 1) * HALF, :].rearrange("p j t -> p (j t)"))
-            score = ps.tile([P, I], F32, name="score%d" % h)
-            nc.tensor.matmul_mx(
-                out=score[:],
-                lhsT=ha_w[:].bitcast(E4M3),
-                lhsT_scale=ha_s[:],
-                rhs=hb_w[:].bitcast(E5M2),
-                rhs_scale=hb_s[:],
-                start=True,
-                stop=True,
+            picked = sb.tile([P, I], F32, name="tv_picked%d" % h, tag="gate_then_tv%d" % h, align_bytes=ALIGN)
+            nc.scalar.activation(picked[:], tv_sb[:, h, :].indirect(tv_list[:]), ACT.Copy)
+            tv_picked.append(picked)
+
+        ha = sb.tile([P, J, PACK], BF16, name="ha", tag="ob_then_ha", align_bytes=ALIGN)
+        for h, rows in halves():
+            nc.vector.tensor_copy(
+                out=ha[:, rows, :].rearrange("p (m n) t -> p m t n", n=STRIDE_READ),
+                in_=ha_flat[:, :, rows].rearrange("p t (m n) -> p m t n", n=STRIDE_READ),
             )
-            bent = sb.tile([P, I], F32, name="bent%d" % h, align_bytes=64)
-            nc.scalar.activation(bent[:], score[:], ACT.Tanh, scale=0.04)
-            y = sb.tile([P, I], F32, name="y%d" % h, align_bytes=64)
-            nc.vector.tensor_tensor(out=y[:], in0=bent[:], in1=tv_g[h][:], op=ALU.mult)
-            nc.sync.dma_start(out=out[h * HALF : (h + 1) * HALF, :], in_=y[:])
+
+        for h, rows in halves():
+            ha_w = sb.tile([P, HALF], U32, name="ha_w%d" % h, align_bytes=ALIGN)
+            ha_s = sb.tile([P, HALF], U8, name="ha_s%d" % h, align_bytes=ALIGN)
+            nc.vector.quantize_mx(
+                out=ha_w[:].bitcast(E4M3), scales=ha_s[:], in_=ha[:, rows, :].rearrange("p j t -> p (j t)")
+            )
+            if h == 0:
+                quantize_hb(second_cols)
+            y = sb.tile([P, I], F32, name="y%d" % h, align_bytes=ALIGN)
+            for c, cols in halves():
+                score = ps.tile([P, HALF], F32, name="score%d%d" % (h, c))
+                nc.tensor.matmul_mx(
+                    out=score[:],
+                    lhsT=ha_w[:].bitcast(E4M3),
+                    lhsT_scale=ha_s[:],
+                    rhs=hb_w[:, cols].bitcast(E5M2),
+                    rhs_scale=hb_s[:, cols],
+                    start=True,
+                    stop=True,
+                )
+                bent = sb.tile([P, HALF], F32, name="bent%d%d" % (h, c), align_bytes=ALIGN)
+                nc.scalar.activation(bent[:], score[:], ACT.Tanh, scale=0.04)
+                nc.vector.tensor_tensor(out=y[:, cols], in0=bent[:], in1=tv_picked[h][:, cols], op=ALU.mult)
+            nc.sync.dma_start(out=out[rows, :], in_=y[:])

from contextlib import ExitStack

import concourse.mybir as mybir

K, T, J, I, R, Q = 512, 512, 256, 256, 512, 512
FLOPS = 2 * K * R * J + 2 * K * R * I + 2 * R * J * I

F32 = mybir.dt.float32
BF16 = mybir.dt.bfloat16
I32 = mybir.dt.int32
U32 = mybir.dt.uint32
U16 = mybir.dt.uint16
U8 = mybir.dt.uint8
E4M3 = mybir.dt.float8_e4m3fn_x4
E5M2 = mybir.dt.float8_e5m2_x4
E2M1 = mybir.dt.float4_e2m1fn_x4
ACT = mybir.ActivationFunctionType
ALU = mybir.AluOpType

P = 128
PACK = 4
RUN = 4
HALF = 128
LIST_ROWS = 16
ALIGN = 64
STRIDE_READ = 4


def halves():
    return [(h, slice(h * HALF, (h + 1) * HALF)) for h in range(2)]


def load_scale_rows(queues, plane, scales):
    rows = scales[0].bitcast(I32)
    for n in range(4):
        queues[n % len(queues)].dma_start(out=plane[32 * n : 32 * n + 4, :], in_=rows[4 * n : 4 * n + 4, :])


def deal_columns(nc, dealt, raw, words_per_run):
    nc.vector.tensor_copy(
        out=dealt.rearrange("p (t g w) -> p g t w", t=PACK, w=words_per_run),
        in_=raw.rearrange("p (g t w) -> p g t w", t=PACK, w=words_per_run),
    )


def tile_list_meet_peakgated_added_tabled_kernel(
    tc, xt_words, xt_scales, wa_words, wa_scales, wb_words, wb_scales, ob, tv, offs, offs2, offs3, out
):
    nc = tc.nc
    with ExitStack() as ctx:
        sb = ctx.enter_context(tc.tile_pool(name="sb", bufs=1))
        ps = ctx.enter_context(tc.psum_pool(name="ps", bufs=1))

        rows_list = sb.tile([P, J // LIST_ROWS], U16, name="rows_list")
        cols_list = sb.tile([P, I // LIST_ROWS], U16, name="cols_list")
        tv_list = sb.tile([P, I // LIST_ROWS], U16, name="tv_list")
        xt_w = sb.tile([P, T], I32, name="xt_w", align_bytes=ALIGN)
        xt_s = sb.tile([P, T // 4], I32, name="xt_s", align_bytes=ALIGN)
        wa_w_raw = sb.tile([P, R // 2], I32, name="wa_w_raw", align_bytes=ALIGN)
        wb_w_raw = sb.tile([P, R], I32, name="wb_w_raw", align_bytes=ALIGN)
        wa_s_raw = sb.tile([P, R // 4], I32, name="wa_s_raw", tag="wa_s_raw_then_xb_s", align_bytes=ALIGN)
        wb_s_raw = sb.tile([P, R // 4], I32, name="wb_s_raw", tag="wb_s_raw_then_peak", align_bytes=ALIGN)
        ob_sb = sb.tile([P, PACK, I], F32, name="ob_sb", tag="ob_then_ha", align_bytes=ALIGN)
        tv_sb = sb.tile([P, 2, Q], F32, name="tv_sb", align_bytes=ALIGN)

        nc.vector.memset(xt_s[:], 0)
        nc.gpsimd.memset(wa_s_raw[:], 0)
        nc.gpsimd.memset(wb_s_raw[:], 0)

        nc.sync.dma_start(rows_list[:], offs)
        nc.scalar.dma_start(out=xt_w[:], in_=xt_words[0].rearrange("p n t -> p (n t)").bitcast(I32))
        nc.sync.dma_start(cols_list[:], offs2)
        nc.scalar.dma_start(out=wa_w_raw[:], in_=wa_words[0].bitcast(I32))
        load_scale_rows([nc.sync, nc.scalar], xt_s, xt_scales)
        load_scale_rows([nc.sync, nc.scalar, nc.sync, nc.gpsimd], wa_s_raw, wa_scales)
        load_scale_rows([nc.scalar, nc.sync], wb_s_raw, wb_scales)
        nc.scalar.dma_start(out=wb_w_raw[:], in_=wb_words[0].rearrange("p n t -> p (n t)").bitcast(I32))
        ob_runs = ob.rearrange("(g t e) i -> e g t i", t=PACK, e=RUN)
        for e, queue in enumerate([nc.sync, nc.sync, nc.sync, nc.gpsimd]):
            queue.dma_start(out=ob_sb[e:P:RUN, :, :], in_=ob_runs[e])
        nc.sync.dma_start(tv_list[:], offs3)
        nc.sync.dma_start(out=tv_sb[:], in_=tv.rearrange("(h p) q -> p h q", p=P))

        xa_w = sb.tile([P, J], U32, name="xa_w", align_bytes=ALIGN)
        xa_s = sb.tile([P, J], U8, name="xa_s", align_bytes=ALIGN)
        xb_w = sb.tile([P, I], U32, name="xb_w", align_bytes=ALIGN)
        wa_w = sb.tile([P, R // 2], I32, name="wa_w", align_bytes=ALIGN)
        wb_w = sb.tile([P, R], I32, name="wb_w", align_bytes=ALIGN)
        wa_s = sb.tile([P, R // 4], I32, name="wa_s", align_bytes=ALIGN)
        wb_s = sb.tile([P, R // 4], I32, name="wb_s", align_bytes=ALIGN)

        nc.vector.tensor_copy(xa_w[:], xt_w[:].bitcast(U32).indirect(rows_list[:]))
        nc.vector.tensor_copy(xb_w[:], xt_w[:].bitcast(U32).indirect(cols_list[:]))
        nc.vector.tensor_copy(xa_s[:], xt_s[:].bitcast(U8).indirect(rows_list[:]))
        deal_columns(nc, wa_w[:], wa_w_raw[:], RUN // 2)
        deal_columns(nc, wa_s[:], wa_s_raw[:], RUN // 4)
        xb_s = sb.tile([P, I], U8, name="xb_s", tag="wa_s_raw_then_xb_s", align_bytes=ALIGN)
        nc.vector.tensor_copy(xb_s[:], xt_s[:].bitcast(U8).indirect(cols_list[:]))
        deal_columns(nc, wb_s[:], wb_s_raw[:], RUN // 4)
        deal_columns(nc, wb_w[:], wb_w_raw[:], RUN)

        za = [ps.tile([P, 2, J], F32, name="za%d" % b) for b in range(2)]
        for t in range(PACK):
            nc.tensor.matmul_mx(
                out=za[t // 2][:, t % 2, :],
                lhsT=wa_w[:].bitcast(U8)[:, 2 * P * t : 2 * P * (t + 1)].bitcast(E2M1),
                lhsT_scale=wa_s[:].bitcast(U8)[:, P * t : P * (t + 1)],
                rhs=xa_w[:].bitcast(E4M3),
                rhs_scale=xa_s[:],
                start=True,
                stop=True,
            )
        zb = [ps.tile([P, PACK, HALF], F32, name="zb%d" % c) for c in range(2)]
        for c, cols in halves():
            for t in range(PACK):
                nc.tensor.matmul_mx(
                    out=zb[c][:, t, :],
                    lhsT=wb_w[:, P * t : P * (t + 1)].bitcast(E5M2),
                    lhsT_scale=wb_s[:].bitcast(U8)[:, P * t : P * (t + 1)],
                    rhs=xb_w[:, cols].bitcast(E4M3),
                    rhs_scale=xb_s[:, cols],
                    start=True,
                    stop=True,
                )

        ha_flat = sb.tile([P, PACK, J], BF16, name="ha_flat", align_bytes=ALIGN)
        peak = sb.tile([P, PACK], F32, name="peak", tag="wb_s_raw_then_peak", align_bytes=ALIGN)
        gates = []
        for b in range(2):
            gate = sb.tile([P, 2], F32, name="gate%d" % b, tag="gate_then_tv%d" % b, align_bytes=ALIGN)
            nc.vector.tensor_reduce(out=peak[:, 2 * b : 2 * b + 2], in_=za[b][:], axis=mybir.AxisListType.X, op=ALU.max)
            nc.scalar.mul(gate[:], peak[:, 2 * b : 2 * b + 2], -0.4)
            gates.append(gate)
        for t in range(PACK):
            b, u = divmod(t, 2)
            nc.scalar.activation(ha_flat[:, t, :], za[b][:, u, :], ACT.Relu, bias=gates[b][:, u : u + 1])

        hb = sb.tile([P, I, PACK], BF16, name="hb", align_bytes=ALIGN)
        for c, cols in halves():
            nc.vector.tensor_tensor(
                out=hb[:, cols, :].rearrange("p (m n) t -> p m t n", n=STRIDE_READ),
                in0=zb[c][:].rearrange("p t (m n) -> p m t n", n=STRIDE_READ),
                in1=ob_sb[:, :, cols].rearrange("p t (m n) -> p m t n", n=STRIDE_READ),
                op=ALU.max,
            )
        hb_w = sb.tile([P, I], U32, name="hb_w", align_bytes=ALIGN)
        hb_s = sb.tile([P, I], U8, name="hb_s", align_bytes=ALIGN)

        def quantize_hb(cols):
            nc.vector.quantize_mx(
                out=hb_w[:, cols].bitcast(E5M2), scales=hb_s[:, cols], in_=hb[:, cols, :].rearrange("p i t -> p (i t)")
            )

        first_cols, second_cols = [cols for c, cols in halves()]
        quantize_hb(first_cols)

        tv_picked = []
        for h in range(2):
            picked = sb.tile([P, I], F32, name="tv_picked%d" % h, tag="gate_then_tv%d" % h, align_bytes=ALIGN)
            nc.scalar.activation(picked[:], tv_sb[:, h, :].indirect(tv_list[:]), ACT.Copy)
            tv_picked.append(picked)

        ha = sb.tile([P, J, PACK], BF16, name="ha", tag="ob_then_ha", align_bytes=ALIGN)
        for h, rows in halves():
            nc.vector.tensor_copy(
                out=ha[:, rows, :].rearrange("p (m n) t -> p m t n", n=STRIDE_READ),
                in_=ha_flat[:, :, rows].rearrange("p t (m n) -> p m t n", n=STRIDE_READ),
            )

        for h, rows in halves():
            ha_w = sb.tile([P, HALF], U32, name="ha_w%d" % h, align_bytes=ALIGN)
            ha_s = sb.tile([P, HALF], U8, name="ha_s%d" % h, align_bytes=ALIGN)
            nc.vector.quantize_mx(
                out=ha_w[:].bitcast(E4M3), scales=ha_s[:], in_=ha[:, rows, :].rearrange("p j t -> p (j t)")
            )
            if h == 0:
                quantize_hb(second_cols)
            y = sb.tile([P, I], F32, name="y%d" % h, align_bytes=ALIGN)
            for c, cols in halves():
                score = ps.tile([P, HALF], F32, name="score%d%d" % (h, c))
                nc.tensor.matmul_mx(
                    out=score[:],
                    lhsT=ha_w[:].bitcast(E4M3),
                    lhsT_scale=ha_s[:],
                    rhs=hb_w[:, cols].bitcast(E5M2),
                    rhs_scale=hb_s[:, cols],
                    start=True,
                    stop=True,
                )
                bent = sb.tile([P, HALF], F32, name="bent%d%d" % (h, c), align_bytes=ALIGN)
                nc.scalar.activation(bent[:], score[:], ACT.Tanh, scale=0.04)
                nc.vector.tensor_tensor(out=y[:, cols], in0=bent[:], in1=tv_picked[h][:, cols], op=ALU.mult)
            nc.sync.dma_start(out=out[rows, :], in_=y[:])
